import numpy as np
CORES = [40,64,80,88,96,104,120,144]
N = 8
TIMES = 1
def setup_inputs(rng):
    x = (rng.standard_normal((N, 128, 128), dtype=np.float32) / np.float32(np.sqrt(512 * N)))
    return {"x": x, "xt": x.transpose(0, 2, 1).copy()}
def setup_inputs_big(rng):
    d = setup_inputs(rng)
    for k in ("x", "xt"): d[k] = (d[k].astype(np.float32) * 1024.0).astype(d[k].dtype)
    return d
def setup_inputs_small(rng):
    d = setup_inputs(rng)
    for k in ("x", "xt"): d[k] = (d[k].astype(np.float32) * (1 / 1024.0)).astype(d[k].dtype)
    return d
def setup_inputs_apart(rng):
    d = setup_inputs(rng)
    f = (10.0 ** rng.permutation(np.linspace(-1.5, 1.5, N))).astype(np.float32).reshape(N, 1, 1)
    for k in ("x", "xt"): d[k] = (d[k].astype(np.float32) * f).astype(d[k].dtype)
    return d
def reference(x, xt):
    X = list(x.astype(np.float64))
    for _ in range(TIMES):
        G = sum(a.T @ a for a in X)
        X = [1.5 * a - 0.5 * (a @ G) for a in X]
    return {"y": np.stack(X).astype(np.float32)}

@@ -1,0 +1,141 @@
+from concourse.bass import DstId, RemoteDMATransfer
+from concourse.mybir import AluOpType
+
+D = 128
+WORLD = 256
+
+SCRATCH = {
+    "xs": ("sbuf", [D, D], "float32"),
+    "xts": ("sbuf", [D, D], "float32"),
+    "cm": ("sbuf", [D, D], "float32"),
+    "cp": ("sbuf", [D, D], "float32"),
+    "x15": ("sbuf", [D, D], "float32"),
+    "hs": ("sbuf", [D, D], "float32"),
+    "land": ("sbuf", [D, 4 * D], "float32"),
+    "hown": ("sbuf", [D, D], "float32"),
+    "hoth": ("sbuf", [D, D], "float32"),
+    "ys": ("sbuf", [D, D], "float32"),
+    "pg": ("psum", [D, 512], "float32"),
+    "py": ("psum", [D, 512], "float32"),
+}
+SEMAPHORES = ["ldx", "ldxt", "fill", "mm", "cpy", "sc", "sent", "arr", "aown", "aoth", "mm2", "yr", "st"]
+
+
+def _bits(mask, n, avoid=0):
+    out, k = 0, 0
+    for b in range(mask.bit_length()):
+        if k < n and (mask >> b) & 1 and not (avoid >> b) & 1:
+            out |= 1 << b
+            k += 1
+    return out
+
+
+def _count(mask):
+    return bin(mask).count("1")
+
+
+def _plan(T, topo):
+    planes = []
+    for c in T.cores:
+        for p in planes:
+            if topo.same_plane(p[0], c):
+                p.append(c)
+                break
+        else:
+            planes.append([c])
+    a_side, b_side = planes
+    partner = {}
+    for a in a_side:
+        for b in b_side:
+            if topo.mates(a, b):
+                partner[a], partner[b] = b, a
+    rest_a = [a for a in a_side if a not in partner]
+    rest_b = [b for b in b_side if b not in partner]
+    for a, b in zip(rest_a, rest_b):
+        partner[a], partner[b] = b, a
+    red = {}
+    for c in T.cores:
+        red[c] = [w for w in range(WORLD)
+                  if w != c and topo.host(w) == topo.host(c) and topo.chip(w) == topo.chip(c)
+                  and topo.die(w) == topo.die(c) and topo.may_write(w, partner[c])][0]
+    return planes, partner, red
+
+
+def _dst(topo, dst, src):
+    rid, pid = topo.addr(dst, src)
+    return DstId(rid=rid, pnc=pid)
+
+
+def rank_program(g, core, T, topo):
+    planes, partner, red = _plan(T, topo)
+    s = T.sem
+    owner = {red[c]: c for c in T.cores}
+
+    def share_mask(src):
+        plane = [p for p in planes if src in p][0]
+        other = [c for c in plane if c != src][0]
+        return topo.mask(src, red[other])
+
+    if core in owner:
+        mine = owner[core]
+        plane = [p for p in planes if mine in p][0]
+        g.wait_ge(s.arr, sum(_count(share_mask(c)) for c in plane))
+        m = topo.mask(core, partner[mine]) & topo.mask(core, mine)
+        srcs = [T.land[:, k * D:(k + 1) * D] for k in range(len(plane))]
+        half = _count(m) // 2
+        m_far = _bits(m, half)
+        m_near = _bits(m, half, avoid=m_far)
+        g.remote_dma_fused([
+            RemoteDMATransfer(dst_ids=[_dst(topo, partner[mine], core)], dma_engine_mask=m_far, remote_sem=s.aoth,
+                              srcs=srcs, dsts=[T.hoth[:]], alu_op=1),
+            RemoteDMATransfer(dst_ids=[_dst(topo, mine, core)], dma_engine_mask=m_near, remote_sem=s.aown,
+                              srcs=srcs, dsts=[T.hown[:]], alu_op=1),
+        ], local_sem=s.sent)
+        g.wait_ge(s.sent, _count(m_far) + _count(m_near))
+        return
+
+    if T.rank_of(core) is None:
+        return
+
+    plane = [p for p in planes if core in p][0]
+    me = plane.index(core)
+    n = len(plane)
+    g.sync.dma_start(T.xs[:], T.x[:]).then_inc(s.ldx, 16)
+    g.sync.dma_start(T.xts[:], T.xt[:]).then_inc(s.ldxt, 16)
+    g.vector.memset(T.cm[:], -0.5).then_inc(s.fill, 1)
+    g.vector.memset(T.cp[:], 1.5).then_inc(s.fill, 1)
+
+    g.tensor.wait_ge(s.ldx, 16)
+    g.tensor.matmul(T.pg[:, 0:D], T.xs[:], T.xs[:], start=True, stop=True).then_inc(s.mm, 1)
+    g.vector.wait_ge(s.fill, 2)
+    g.vector.wait_ge(s.mm, 1)
+    g.vector.tensor_tensor(T.hs[:], T.pg[:, 0:D], T.cm[:], AluOpType.mult).then_inc(s.cpy, 1)
+
+    order = [plane[(me + k) % n] for k in range(1, n + 1)]
+    m = share_mask(core)
+    g.wait_ge(s.cpy, 1)
+    g.remote_dma_fused([
+        RemoteDMATransfer(dst_ids=[_dst(topo, red[c], core) for c in order], dma_engine_mask=m, remote_sem=s.arr,
+                          srcs=[T.hs[:]], dsts=[T.land[:, me * D:(me + 1) * D] for c in order], alu_op=0),
+    ], local_sem=s.sent)
+
+    g.vector.wait_ge(s.ldx, 16)
+    g.vector.tensor_tensor(T.x15[:], T.xs[:], T.cp[:], AluOpType.mult).then_inc(s.sc, 1)
+
+    r_near = red[core]
+    r_far = red[partner[core]]
+    mm_near = topo.mask(r_near, partner[core]) & topo.mask(r_near, core)
+    mm_far = topo.mask(r_far, core) & topo.mask(r_far, partner[core])
+    g.tensor.wait_ge(s.ldxt, 16)
+    g.tensor.wait_ge(s.aown, _count(mm_near) // 2)
+    g.tensor.matmul(T.py[:, 0:D], T.xts[:], T.hown[:], start=True, stop=False)
+    g.tensor.wait_ge(s.aoth, _count(mm_far) // 2)
+    g.tensor.matmul(T.py[:, 0:D], T.xts[:], T.hoth[:], start=False, stop=True).then_inc(s.mm2, 1)
+
+    g.vector.wait_ge(s.sc, 1)
+    g.vector.wait_ge(s.mm2, 1)
+    g.vector.tensor_tensor(T.ys[:], T.py[:, 0:D], T.x15[:], AluOpType.add).then_inc(s.yr, 1)
+    g.sync.wait_ge(s.yr, 1)
+    g.sync.dma_start(T.y[:], T.ys[:]).then_inc(s.st, 16)
+    g.sync.wait_ge(s.st, 16)
+    g.wait_ge(s.sent, _count(m))

@@ -3,6 +3,11 @@ from concourse.mybir import AluOpType
 
 D = 128
 WORLD = 256
+RANK_FAR = 8
+RANK_NEAR = 4
+RED_FAR = 8
+RED_NEAR = 8
+RED_NEAR_OWN = True
 
 SCRATCH = {
     "xs": ("sbuf", [D, D], "float32"),
@@ -28,10 +33,6 @@ def _bits(mask, n, avoid=0):
             out |= 1 << b
             k += 1
     return out
-
-
-def _count(mask):
-    return bin(mask).count("1")
 
 
 def _plan(T, topo):
@@ -71,27 +72,21 @@ def rank_program(g, core, T, topo):
     s = T.sem
     owner = {red[c]: c for c in T.cores}
 
-    def share_mask(src):
-        plane = [p for p in planes if src in p][0]
-        other = [c for c in plane if c != src][0]
-        return topo.mask(src, red[other])
-
     if core in owner:
         mine = owner[core]
         plane = [p for p in planes if mine in p][0]
-        g.wait_ge(s.arr, sum(_count(share_mask(c)) for c in plane))
-        m = topo.mask(core, partner[mine]) & topo.mask(core, mine)
+        g.wait_ge(s.arr, (len(plane) - 1) * RANK_FAR + (RANK_NEAR or RANK_FAR))
+        far = topo.mask(core, partner[mine])
+        m_far = _bits(far, RED_FAR)
+        m_near = _bits(topo.mask(core, mine), RED_NEAR, avoid=far if RED_NEAR_OWN else m_far)
         srcs = [T.land[:, k * D:(k + 1) * D] for k in range(len(plane))]
-        half = _count(m) // 2
-        m_far = _bits(m, half)
-        m_near = _bits(m, half, avoid=m_far)
         g.remote_dma_fused([
             RemoteDMATransfer(dst_ids=[_dst(topo, partner[mine], core)], dma_engine_mask=m_far, remote_sem=s.aoth,
                               srcs=srcs, dsts=[T.hoth[:]], alu_op=1),
             RemoteDMATransfer(dst_ids=[_dst(topo, mine, core)], dma_engine_mask=m_near, remote_sem=s.aown,
                               srcs=srcs, dsts=[T.hown[:]], alu_op=1),
         ], local_sem=s.sent)
-        g.wait_ge(s.sent, _count(m_far) + _count(m_near))
+        g.wait_ge(s.sent, RED_FAR + RED_NEAR)
         return
 
     if T.rank_of(core) is None:
@@ -111,25 +106,30 @@ def rank_program(g, core, T, topo):
     g.vector.wait_ge(s.mm, 1)
     g.vector.tensor_tensor(T.hs[:], T.pg[:, 0:D], T.cm[:], AluOpType.mult).then_inc(s.cpy, 1)
 
-    order = [plane[(me + k) % n] for k in range(1, n + 1)]
-    m = share_mask(core)
+    away = [plane[(me + k) % n] for k in range(1, n)]
+    far = topo.mask(core, red[away[0]])
+    m_far = _bits(far, RANK_FAR)
+    slot = T.land[:, me * D:(me + 1) * D]
+    if RANK_NEAR:
+        m_near = _bits(topo.mask(core, red[core]), RANK_NEAR, avoid=far)
+        trs = [RemoteDMATransfer(dst_ids=[_dst(topo, red[c], core) for c in away], dma_engine_mask=m_far,
+                                 remote_sem=s.arr, srcs=[T.hs[:]], dsts=[slot for c in away], alu_op=0),
+               RemoteDMATransfer(dst_ids=[_dst(topo, red[core], core)], dma_engine_mask=m_near,
+                                 remote_sem=s.arr, srcs=[T.hs[:]], dsts=[slot], alu_op=0)]
+    else:
+        allr = away + [core]
+        trs = [RemoteDMATransfer(dst_ids=[_dst(topo, red[c], core) for c in allr], dma_engine_mask=m_far,
+                                 remote_sem=s.arr, srcs=[T.hs[:]], dsts=[slot for c in allr], alu_op=0)]
     g.wait_ge(s.cpy, 1)
-    g.remote_dma_fused([
-        RemoteDMATransfer(dst_ids=[_dst(topo, red[c], core) for c in order], dma_engine_mask=m, remote_sem=s.arr,
-                          srcs=[T.hs[:]], dsts=[T.land[:, me * D:(me + 1) * D] for c in order], alu_op=0),
-    ], local_sem=s.sent)
+    g.remote_dma_fused(trs, local_sem=s.sent)
 
     g.vector.wait_ge(s.ldx, 16)
     g.vector.tensor_tensor(T.x15[:], T.xs[:], T.cp[:], AluOpType.mult).then_inc(s.sc, 1)
 
-    r_near = red[core]
-    r_far = red[partner[core]]
-    mm_near = topo.mask(r_near, partner[core]) & topo.mask(r_near, core)
-    mm_far = topo.mask(r_far, core) & topo.mask(r_far, partner[core])
     g.tensor.wait_ge(s.ldxt, 16)
-    g.tensor.wait_ge(s.aown, _count(mm_near) // 2)
+    g.tensor.wait_ge(s.aown, RED_NEAR)
     g.tensor.matmul(T.py[:, 0:D], T.xts[:], T.hown[:], start=True, stop=False)
-    g.tensor.wait_ge(s.aoth, _count(mm_far) // 2)
+    g.tensor.wait_ge(s.aoth, RED_FAR)
     g.tensor.matmul(T.py[:, 0:D], T.xts[:], T.hoth[:], start=False, stop=True).then_inc(s.mm2, 1)
 
     g.vector.wait_ge(s.sc, 1)
@@ -138,4 +138,4 @@ def rank_program(g, core, T, topo):
     g.sync.wait_ge(s.yr, 1)
     g.sync.dma_start(T.y[:], T.ys[:]).then_inc(s.st, 16)
     g.sync.wait_ge(s.st, 16)
-    g.wait_ge(s.sent, _count(m))
+    g.wait_ge(s.sent, RANK_FAR + RANK_NEAR)

@@ -4,10 +4,9 @@ from concourse.mybir import AluOpType
 D = 128
 WORLD = 256
 RANK_FAR = 8
-RANK_NEAR = 4
+RANK_NEAR = 8
 RED_FAR = 8
 RED_NEAR = 8
-RED_NEAR_OWN = True
 
 SCRATCH = {
     "xs": ("sbuf", [D, D], "float32"),
@@ -18,12 +17,13 @@ SCRATCH = {
     "hs": ("sbuf", [D, D], "float32"),
     "land": ("sbuf", [D, 4 * D], "float32"),
     "hown": ("sbuf", [D, D], "float32"),
+    "hone": ("sbuf", [D, D], "float32"),
     "hoth": ("sbuf", [D, D], "float32"),
     "ys": ("sbuf", [D, D], "float32"),
     "pg": ("psum", [D, 512], "float32"),
     "py": ("psum", [D, 512], "float32"),
 }
-SEMAPHORES = ["ldx", "ldxt", "fill", "mm", "cpy", "sc", "sent", "arr", "aown", "aoth", "mm2", "yr", "st"]
+SEMAPHORES = ["ldx", "ldxt", "fill", "mm", "cpy", "sc", "sent", "arr", "arn", "aown", "aone", "aoth", "mm2", "yr", "st"]
 
 
 def _bits(mask, n, avoid=0):
@@ -75,18 +75,22 @@ def rank_program(g, core, T, topo):
     if core in owner:
         mine = owner[core]
         plane = [p for p in planes if mine in p][0]
-        g.wait_ge(s.arr, (len(plane) - 1) * RANK_FAR + (RANK_NEAR or RANK_FAR))
+        k_mine = plane.index(mine)
         far = topo.mask(core, partner[mine])
         m_far = _bits(far, RED_FAR)
-        m_near = _bits(topo.mask(core, mine), RED_NEAR, avoid=far if RED_NEAR_OWN else m_far)
-        srcs = [T.land[:, k * D:(k + 1) * D] for k in range(len(plane))]
+        m_near = _bits(topo.mask(core, mine), RED_NEAR, avoid=far)
+        slots = [T.land[:, k * D:(k + 1) * D] for k in range(len(plane))]
+        rid, pid = topo.addr(partner[mine], core)
+        g.wait_ge(s.arn, RANK_NEAR)
+        g.remote_dma(T.hone[:], slots[k_mine], s.aone, s.sent, pid, rid, m_far)
+        g.wait_ge(s.arr, (len(plane) - 1) * RANK_FAR)
         g.remote_dma_fused([
-            RemoteDMATransfer(dst_ids=[_dst(topo, partner[mine], core)], dma_engine_mask=m_far, remote_sem=s.aoth,
-                              srcs=srcs, dsts=[T.hoth[:]], alu_op=1),
+            RemoteDMATransfer(dst_ids=[DstId(rid=rid, pnc=pid)], dma_engine_mask=m_far, remote_sem=s.aoth,
+                              srcs=[a for k, a in enumerate(slots) if k != k_mine], dsts=[T.hoth[:]], alu_op=1),
             RemoteDMATransfer(dst_ids=[_dst(topo, mine, core)], dma_engine_mask=m_near, remote_sem=s.aown,
-                              srcs=srcs, dsts=[T.hown[:]], alu_op=1),
+                              srcs=slots, dsts=[T.hown[:]], alu_op=1),
         ], local_sem=s.sent)
-        g.wait_ge(s.sent, RED_FAR + RED_NEAR)
+        g.wait_ge(s.sent, 2 * RED_FAR + RED_NEAR)
         return
 
     if T.rank_of(core) is None:
@@ -109,26 +113,24 @@ def rank_program(g, core, T, topo):
     away = [plane[(me + k) % n] for k in range(1, n)]
     far = topo.mask(core, red[away[0]])
     m_far = _bits(far, RANK_FAR)
+    m_near = _bits(topo.mask(core, red[core]), RANK_NEAR, avoid=far)
     slot = T.land[:, me * D:(me + 1) * D]
-    if RANK_NEAR:
-        m_near = _bits(topo.mask(core, red[core]), RANK_NEAR, avoid=far)
-        trs = [RemoteDMATransfer(dst_ids=[_dst(topo, red[c], core) for c in away], dma_engine_mask=m_far,
-                                 remote_sem=s.arr, srcs=[T.hs[:]], dsts=[slot for c in away], alu_op=0),
-               RemoteDMATransfer(dst_ids=[_dst(topo, red[core], core)], dma_engine_mask=m_near,
-                                 remote_sem=s.arr, srcs=[T.hs[:]], dsts=[slot], alu_op=0)]
-    else:
-        allr = away + [core]
-        trs = [RemoteDMATransfer(dst_ids=[_dst(topo, red[c], core) for c in allr], dma_engine_mask=m_far,
-                                 remote_sem=s.arr, srcs=[T.hs[:]], dsts=[slot for c in allr], alu_op=0)]
     g.wait_ge(s.cpy, 1)
-    g.remote_dma_fused(trs, local_sem=s.sent)
+    g.remote_dma_fused([
+        RemoteDMATransfer(dst_ids=[_dst(topo, red[c], core) for c in away], dma_engine_mask=m_far,
+                          remote_sem=s.arr, srcs=[T.hs[:]], dsts=[slot for c in away], alu_op=0),
+        RemoteDMATransfer(dst_ids=[_dst(topo, red[core], core)], dma_engine_mask=m_near,
+                          remote_sem=s.arn, srcs=[T.hs[:]], dsts=[slot], alu_op=0),
+    ], local_sem=s.sent)
 
     g.vector.wait_ge(s.ldx, 16)
     g.vector.tensor_tensor(T.x15[:], T.xs[:], T.cp[:], AluOpType.mult).then_inc(s.sc, 1)
 
     g.tensor.wait_ge(s.ldxt, 16)
+    g.tensor.wait_ge(s.aone, RED_FAR)
+    g.tensor.matmul(T.py[:, 0:D], T.xts[:], T.hone[:], start=True, stop=False)
     g.tensor.wait_ge(s.aown, RED_NEAR)
-    g.tensor.matmul(T.py[:, 0:D], T.xts[:], T.hown[:], start=True, stop=False)
+    g.tensor.matmul(T.py[:, 0:D], T.xts[:], T.hown[:], start=False, stop=False)
     g.tensor.wait_ge(s.aoth, RED_FAR)
     g.tensor.matmul(T.py[:, 0:D], T.xts[:], T.hoth[:], start=False, stop=True).then_inc(s.mm2, 1)
 

@@ -15,15 +15,20 @@ SCRATCH = {
     "cp": ("sbuf", [D, D], "float32"),
     "x15": ("sbuf", [D, D], "float32"),
     "hs": ("sbuf", [D, D], "float32"),
-    "land": ("sbuf", [D, 4 * D], "float32"),
+    "lx0": ("sbuf", [D, D], "float32"),
+    "lx1": ("sbuf", [D, D], "float32"),
+    "land": ("sbuf", [D, 2 * D], "float32"),
+    "xp": ("sbuf", [D, D], "float32"),
+    "hp": ("sbuf", [D, D], "float32"),
     "hown": ("sbuf", [D, D], "float32"),
-    "hone": ("sbuf", [D, D], "float32"),
     "hoth": ("sbuf", [D, D], "float32"),
     "ys": ("sbuf", [D, D], "float32"),
     "pg": ("psum", [D, 512], "float32"),
+    "pq": ("psum", [D, 512], "float32"),
     "py": ("psum", [D, 512], "float32"),
 }
-SEMAPHORES = ["ldx", "ldxt", "fill", "mm", "cpy", "sc", "sent", "arr", "arn", "aown", "aone", "aoth", "mm2", "yr", "st"]
+SEMAPHORES = ["ldx", "ldxt", "fill", "mm", "cpy", "sc", "sent", "arr", "arn", "arx", "axp", "mmq", "cpq",
+              "aown", "aoth", "mm2", "yr", "st"]
 
 
 def _bits(mask, n, avoid=0):
@@ -71,24 +76,30 @@ def rank_program(g, core, T, topo):
     planes, partner, red = _plan(T, topo)
     s = T.sem
     owner = {red[c]: c for c in T.cores}
+    mult = AluOpType.mult
 
     if core in owner:
         mine = owner[core]
-        plane = [p for p in planes if mine in p][0]
-        k_mine = plane.index(mine)
         far = topo.mask(core, partner[mine])
         m_far = _bits(far, RED_FAR)
         m_near = _bits(topo.mask(core, mine), RED_NEAR, avoid=far)
-        slots = [T.land[:, k * D:(k + 1) * D] for k in range(len(plane))]
         rid, pid = topo.addr(partner[mine], core)
+        g.vector.memset(T.cm[:], -0.5).then_inc(s.fill, 1)
         g.wait_ge(s.arn, RANK_NEAR)
-        g.remote_dma(T.hone[:], slots[k_mine], s.aone, s.sent, pid, rid, m_far)
-        g.wait_ge(s.arr, (len(plane) - 1) * RANK_FAR)
+        g.remote_dma(T.xp[:], T.lx0[:], s.axp, s.sent, pid, rid, m_far)
+        g.tensor.wait_ge(s.arx, RANK_FAR)
+        g.tensor.matmul(T.pg[:, 0:D], T.lx1[:], T.lx1[:], start=True, stop=True).then_inc(s.mm, 1)
+        g.vector.wait_ge(s.fill, 1)
+        g.vector.wait_ge(s.mm, 1)
+        g.vector.tensor_tensor(T.hs[:], T.pg[:, 0:D], T.cm[:], mult).then_inc(s.cpy, 1)
+        srcs = [T.hs[:], T.land[:, 0:D], T.land[:, D:2 * D]]
+        g.wait_ge(s.cpy, 1)
+        g.wait_ge(s.arr, 2 * RANK_FAR)
         g.remote_dma_fused([
             RemoteDMATransfer(dst_ids=[DstId(rid=rid, pnc=pid)], dma_engine_mask=m_far, remote_sem=s.aoth,
-                              srcs=[a for k, a in enumerate(slots) if k != k_mine], dsts=[T.hoth[:]], alu_op=1),
+                              srcs=srcs, dsts=[T.hoth[:]], alu_op=1),
             RemoteDMATransfer(dst_ids=[_dst(topo, mine, core)], dma_engine_mask=m_near, remote_sem=s.aown,
-                              srcs=slots, dsts=[T.hown[:]], alu_op=1),
+                              srcs=srcs, dsts=[T.hown[:]], alu_op=1),
         ], local_sem=s.sent)
         g.wait_ge(s.sent, 2 * RED_FAR + RED_NEAR)
         return
@@ -104,31 +115,43 @@ def rank_program(g, core, T, topo):
     g.vector.memset(T.cm[:], -0.5).then_inc(s.fill, 1)
     g.vector.memset(T.cp[:], 1.5).then_inc(s.fill, 1)
 
-    g.tensor.wait_ge(s.ldx, 16)
-    g.tensor.matmul(T.pg[:, 0:D], T.xs[:], T.xs[:], start=True, stop=True).then_inc(s.mm, 1)
-    g.vector.wait_ge(s.fill, 2)
-    g.vector.wait_ge(s.mm, 1)
-    g.vector.tensor_tensor(T.hs[:], T.pg[:, 0:D], T.cm[:], AluOpType.mult).then_inc(s.cpy, 1)
-
     away = [plane[(me + k) % n] for k in range(1, n)]
     far = topo.mask(core, red[away[0]])
     m_far = _bits(far, RANK_FAR)
     m_near = _bits(topo.mask(core, red[core]), RANK_NEAR, avoid=far)
-    slot = T.land[:, me * D:(me + 1) * D]
+    g.wait_ge(s.ldx, 16)
+    g.remote_dma_fused([
+        RemoteDMATransfer(dst_ids=[_dst(topo, red[away[0]], core)], dma_engine_mask=m_far,
+                          remote_sem=s.arx, srcs=[T.xs[:]], dsts=[T.lx1[:]], alu_op=0),
+        RemoteDMATransfer(dst_ids=[_dst(topo, red[core], core)], dma_engine_mask=m_near,
+                          remote_sem=s.arn, srcs=[T.xs[:]], dsts=[T.lx0[:]], alu_op=0),
+    ], local_sem=s.sent)
+
+    g.tensor.wait_ge(s.ldx, 16)
+    g.tensor.matmul(T.pg[:, 0:D], T.xs[:], T.xs[:], start=True, stop=True).then_inc(s.mm, 1)
+    g.vector.wait_ge(s.fill, 2)
+    g.vector.wait_ge(s.mm, 1)
+    g.vector.tensor_tensor(T.hs[:], T.pg[:, 0:D], T.cm[:], mult).then_inc(s.cpy, 1)
+
     g.wait_ge(s.cpy, 1)
     g.remote_dma_fused([
-        RemoteDMATransfer(dst_ids=[_dst(topo, red[c], core) for c in away], dma_engine_mask=m_far,
-                          remote_sem=s.arr, srcs=[T.hs[:]], dsts=[slot for c in away], alu_op=0),
-        RemoteDMATransfer(dst_ids=[_dst(topo, red[core], core)], dma_engine_mask=m_near,
-                          remote_sem=s.arn, srcs=[T.hs[:]], dsts=[slot], alu_op=0),
+        RemoteDMATransfer(dst_ids=[_dst(topo, red[c], core) for c in away[1:]], dma_engine_mask=m_far,
+                          remote_sem=s.arr, srcs=[T.hs[:]],
+                          dsts=[T.land[:, k * D:(k + 1) * D] for k in range(n - 2)], alu_op=0),
     ], local_sem=s.sent)
 
     g.vector.wait_ge(s.ldx, 16)
-    g.vector.tensor_tensor(T.x15[:], T.xs[:], T.cp[:], AluOpType.mult).then_inc(s.sc, 1)
+    g.vector.tensor_tensor(T.x15[:], T.xs[:], T.cp[:], mult).then_inc(s.sc, 1)
 
     g.tensor.wait_ge(s.ldxt, 16)
-    g.tensor.wait_ge(s.aone, RED_FAR)
-    g.tensor.matmul(T.py[:, 0:D], T.xts[:], T.hone[:], start=True, stop=False)
+    g.tensor.wait_ge(s.cpy, 1)
+    g.tensor.matmul(T.py[:, 0:D], T.xts[:], T.hs[:], start=True, stop=False)
+    g.tensor.wait_ge(s.axp, RED_FAR)
+    g.tensor.matmul(T.pq[:, 0:D], T.xp[:], T.xp[:], start=True, stop=True).then_inc(s.mmq, 1)
+    g.vector.wait_ge(s.mmq, 1)
+    g.vector.tensor_tensor(T.hp[:], T.pq[:, 0:D], T.cm[:], mult).then_inc(s.cpq, 1)
+    g.tensor.wait_ge(s.cpq, 1)
+    g.tensor.matmul(T.py[:, 0:D], T.xts[:], T.hp[:], start=False, stop=False)
     g.tensor.wait_ge(s.aown, RED_NEAR)
     g.tensor.matmul(T.py[:, 0:D], T.xts[:], T.hown[:], start=False, stop=False)
     g.tensor.wait_ge(s.aoth, RED_FAR)
@@ -140,4 +163,4 @@ def rank_program(g, core, T, topo):
     g.sync.wait_ge(s.yr, 1)
     g.sync.dma_start(T.y[:], T.ys[:]).then_inc(s.st, 16)
     g.sync.wait_ge(s.st, 16)
-    g.wait_ge(s.sent, RANK_FAR + RANK_NEAR)
+    g.wait_ge(s.sent, 2 * RANK_FAR + RANK_NEAR)

@@ -2,33 +2,37 @@ from concourse.bass import DstId, RemoteDMATransfer
 from concourse.mybir import AluOpType
 
 D = 128
+HALF = 64
 WORLD = 256
-RANK_FAR = 8
-RANK_NEAR = 8
-RED_FAR = 8
-RED_NEAR = 8
+NE = 8
 
 SCRATCH = {
+    "xd": ("dram", [D, D], "float32"),
+    "xd0": ("dram", [D, D], "float32"),
     "xs": ("sbuf", [D, D], "float32"),
     "xts": ("sbuf", [D, D], "float32"),
+    "xtm": ("sbuf", [D, D], "float32"),
     "cm": ("sbuf", [D, D], "float32"),
     "cp": ("sbuf", [D, D], "float32"),
     "x15": ("sbuf", [D, D], "float32"),
     "hs": ("sbuf", [D, D], "float32"),
-    "lx0": ("sbuf", [D, D], "float32"),
     "lx1": ("sbuf", [D, D], "float32"),
-    "land": ("sbuf", [D, 2 * D], "float32"),
+    "lh0": ("sbuf", [D, D], "float32"),
+    "land": ("sbuf", [D, D], "float32"),
     "xp": ("sbuf", [D, D], "float32"),
     "hp": ("sbuf", [D, D], "float32"),
+    "hdir": ("sbuf", [D, D], "float32"),
     "hown": ("sbuf", [D, D], "float32"),
     "hoth": ("sbuf", [D, D], "float32"),
     "ys": ("sbuf", [D, D], "float32"),
     "pg": ("psum", [D, 512], "float32"),
-    "pq": ("psum", [D, 512], "float32"),
-    "py": ("psum", [D, 512], "float32"),
+    "pq0": ("psum", [D, 512], "float32"),
+    "pq1": ("psum", [D, 512], "float32"),
+    "py0": ("psum", [D, 512], "float32"),
+    "py1": ("psum", [D, 512], "float32"),
 }
-SEMAPHORES = ["ldx", "ldxt", "fill", "mm", "cpy", "sc", "sent", "arr", "arn", "arx", "axp", "mmq", "cpq",
-              "aown", "aoth", "mm2", "yr", "st"]
+SEMAPHORES = ["ldd", "ldx", "ldxt", "fill", "mm", "cpy", "sc", "sent", "arn", "arx", "arr", "arh", "axp", "adir",
+              "mmq0", "mmq1", "cpq0", "cpq1", "aown", "aoth", "mmy0", "mmy1", "yr0", "yr1", "st"]
 
 
 def _bits(mask, n, avoid=0):
@@ -67,41 +71,44 @@ def _plan(T, topo):
     return planes, partner, red
 
 
-def _dst(topo, dst, src):
-    rid, pid = topo.addr(dst, src)
-    return DstId(rid=rid, pnc=pid)
+def _send(g, topo, core, dst, out, src, rsem, lsem, mask):
+    rid, pid = topo.addr(dst, core)
+    g.remote_dma(out, src, rsem, lsem, pid, rid, mask)
+
+
+def _fold(g, topo, core, dst, out, srcs, rsem, lsem, mask):
+    rid, pid = topo.addr(dst, core)
+    g.remote_dma_fused([RemoteDMATransfer(dst_ids=[DstId(rid=rid, pnc=pid)], dma_engine_mask=mask, remote_sem=rsem,
+                                          srcs=srcs, dsts=[out], alu_op=1)], local_sem=lsem)
 
 
 def rank_program(g, core, T, topo):
     planes, partner, red = _plan(T, topo)
     s = T.sem
     owner = {red[c]: c for c in T.cores}
-    mult = AluOpType.mult
+    mult, add = AluOpType.mult, AluOpType.add
 
     if core in owner:
         mine = owner[core]
+        plane = [p for p in planes if mine in p][0]
+        n = len(plane)
+        ahead = plane[(plane.index(mine) + n - 1) % n]
         far = topo.mask(core, partner[mine])
-        m_far = _bits(far, RED_FAR)
-        m_near = _bits(topo.mask(core, mine), RED_NEAR, avoid=far)
-        rid, pid = topo.addr(partner[mine], core)
-        g.vector.memset(T.cm[:], -0.5).then_inc(s.fill, 1)
-        g.wait_ge(s.arn, RANK_NEAR)
-        g.remote_dma(T.xp[:], T.lx0[:], s.axp, s.sent, pid, rid, m_far)
-        g.tensor.wait_ge(s.arx, RANK_FAR)
+        m_far = _bits(far, NE)
+        m_near = _bits(topo.mask(core, mine), NE, avoid=far)
+        g.wait_ge(s.arn, NE)
+        _send(g, topo, core, partner[ahead], T.xp[:], T.xd0[:], s.axp, s.sent, m_far)
+        g.tensor.wait_ge(s.arx, NE)
         g.tensor.matmul(T.pg[:, 0:D], T.lx1[:], T.lx1[:], start=True, stop=True).then_inc(s.mm, 1)
-        g.vector.wait_ge(s.fill, 1)
+        g.vector.wait_ge(s.arh, NE)
         g.vector.wait_ge(s.mm, 1)
-        g.vector.tensor_tensor(T.hs[:], T.pg[:, 0:D], T.cm[:], mult).then_inc(s.cpy, 1)
-        srcs = [T.hs[:], T.land[:, 0:D], T.land[:, D:2 * D]]
+        g.vector.tensor_tensor(T.hs[:], T.pg[:, 0:D], T.lh0[:], add).then_inc(s.cpy, 1)
+        srcs = [T.hs[:], T.land[:]]
         g.wait_ge(s.cpy, 1)
-        g.wait_ge(s.arr, 2 * RANK_FAR)
-        g.remote_dma_fused([
-            RemoteDMATransfer(dst_ids=[DstId(rid=rid, pnc=pid)], dma_engine_mask=m_far, remote_sem=s.aoth,
-                              srcs=srcs, dsts=[T.hoth[:]], alu_op=1),
-            RemoteDMATransfer(dst_ids=[_dst(topo, mine, core)], dma_engine_mask=m_near, remote_sem=s.aown,
-                              srcs=srcs, dsts=[T.hown[:]], alu_op=1),
-        ], local_sem=s.sent)
-        g.wait_ge(s.sent, 2 * RED_FAR + RED_NEAR)
+        g.wait_ge(s.arr, NE)
+        _fold(g, topo, core, partner[mine], T.hoth[:], srcs, s.aoth, s.sent, m_far)
+        _fold(g, topo, core, mine, T.hown[:], srcs, s.aown, s.sent, m_near)
+        g.wait_ge(s.sent, 3 * NE)
         return
 
     if T.rank_of(core) is None:
@@ -110,57 +117,63 @@ def rank_program(g, core, T, topo):
     plane = [p for p in planes if core in p][0]
     me = plane.index(core)
     n = len(plane)
-    g.sync.dma_start(T.xs[:], T.x[:]).then_inc(s.ldx, 16)
+    away = [plane[(me + k) % n] for k in range(1, n)]
+    far = topo.mask(core, red[away[0]])
+    m_far = _bits(far, NE)
+    m_near = _bits(topo.mask(core, red[core]), NE, avoid=far)
+
+    g.sync.dma_start(T.xd[:], T.x[:]).then_inc(s.ldd, 16)
+    g.scalar.dma_start(T.xs[:], T.x[:]).then_inc(s.ldx, 16)
     g.sync.dma_start(T.xts[:], T.xt[:]).then_inc(s.ldxt, 16)
     g.vector.memset(T.cm[:], -0.5).then_inc(s.fill, 1)
     g.vector.memset(T.cp[:], 1.5).then_inc(s.fill, 1)
 
-    away = [plane[(me + k) % n] for k in range(1, n)]
-    far = topo.mask(core, red[away[0]])
-    m_far = _bits(far, RANK_FAR)
-    m_near = _bits(topo.mask(core, red[core]), RANK_NEAR, avoid=far)
-    g.wait_ge(s.ldx, 16)
-    g.remote_dma_fused([
-        RemoteDMATransfer(dst_ids=[_dst(topo, red[away[0]], core)], dma_engine_mask=m_far,
-                          remote_sem=s.arx, srcs=[T.xs[:]], dsts=[T.lx1[:]], alu_op=0),
-        RemoteDMATransfer(dst_ids=[_dst(topo, red[core], core)], dma_engine_mask=m_near,
-                          remote_sem=s.arn, srcs=[T.xs[:]], dsts=[T.lx0[:]], alu_op=0),
-    ], local_sem=s.sent)
+    g.wait_ge(s.ldd, 16)
+    _send(g, topo, core, red[core], T.xd0[:], T.xd[:], s.arn, s.sent, m_far)
+    _send(g, topo, core, red[away[0]], T.lx1[:], T.xd[:], s.arx, s.sent, m_far)
 
     g.tensor.wait_ge(s.ldx, 16)
     g.tensor.matmul(T.pg[:, 0:D], T.xs[:], T.xs[:], start=True, stop=True).then_inc(s.mm, 1)
-    g.vector.wait_ge(s.fill, 2)
     g.vector.wait_ge(s.mm, 1)
-    g.vector.tensor_tensor(T.hs[:], T.pg[:, 0:D], T.cm[:], mult).then_inc(s.cpy, 1)
+    g.vector.tensor_copy(T.hs[:], T.pg[:, 0:D]).then_inc(s.cpy, 1)
 
     g.wait_ge(s.cpy, 1)
-    g.remote_dma_fused([
-        RemoteDMATransfer(dst_ids=[_dst(topo, red[c], core) for c in away[1:]], dma_engine_mask=m_far,
-                          remote_sem=s.arr, srcs=[T.hs[:]],
-                          dsts=[T.land[:, k * D:(k + 1) * D] for k in range(n - 2)], alu_op=0),
-    ], local_sem=s.sent)
+    _send(g, topo, core, red[away[1]], T.land[:], T.hs[:], s.arr, s.sent, m_far)
+    _send(g, topo, core, red[core], T.lh0[:], T.hs[:], s.arh, s.sent, m_near)
+    _send(g, topo, core, away[2], T.hdir[:], T.hs[:], s.adir, s.sent, m_far)
 
+    g.vector.wait_ge(s.fill, 2)
+    g.vector.wait_ge(s.ldxt, 16)
+    g.vector.tensor_tensor(T.xtm[:], T.xts[:], T.cm[:], mult).then_inc(s.sc, 1)
     g.vector.wait_ge(s.ldx, 16)
     g.vector.tensor_tensor(T.x15[:], T.xs[:], T.cp[:], mult).then_inc(s.sc, 1)
 
-    g.tensor.wait_ge(s.ldxt, 16)
-    g.tensor.wait_ge(s.cpy, 1)
-    g.tensor.matmul(T.py[:, 0:D], T.xts[:], T.hs[:], start=True, stop=False)
-    g.tensor.wait_ge(s.axp, RED_FAR)
-    g.tensor.matmul(T.pq[:, 0:D], T.xp[:], T.xp[:], start=True, stop=True).then_inc(s.mmq, 1)
-    g.vector.wait_ge(s.mmq, 1)
-    g.vector.tensor_tensor(T.hp[:], T.pq[:, 0:D], T.cm[:], mult).then_inc(s.cpq, 1)
-    g.tensor.wait_ge(s.cpq, 1)
-    g.tensor.matmul(T.py[:, 0:D], T.xts[:], T.hp[:], start=False, stop=False)
-    g.tensor.wait_ge(s.aown, RED_NEAR)
-    g.tensor.matmul(T.py[:, 0:D], T.xts[:], T.hown[:], start=False, stop=False)
-    g.tensor.wait_ge(s.aoth, RED_FAR)
-    g.tensor.matmul(T.py[:, 0:D], T.xts[:], T.hoth[:], start=False, stop=True).then_inc(s.mm2, 1)
-
-    g.vector.wait_ge(s.sc, 1)
-    g.vector.wait_ge(s.mm2, 1)
-    g.vector.tensor_tensor(T.ys[:], T.py[:, 0:D], T.x15[:], AluOpType.add).then_inc(s.yr, 1)
-    g.sync.wait_ge(s.yr, 1)
+    halves = (0, 1)
+    col = [slice(h * HALF, (h + 1) * HALF) for h in halves]
+    pq = [T.pq0, T.pq1]
+    py = [T.py0, T.py1]
+    g.tensor.wait_ge(s.sc, 2)
+    g.tensor.wait_ge(s.adir, NE)
+    for h in halves:
+        g.tensor.matmul(py[h][:, 0:HALF], T.xtm[:], T.hdir[:, col[h]], start=True, stop=False)
+    g.tensor.wait_ge(s.axp, NE)
+    for h in halves:
+        g.tensor.matmul(pq[h][:, 0:HALF], T.xp[:], T.xp[:, col[h]], start=True, stop=True).then_inc(s["mmq%d" % h], 1)
+    g.vector.wait_ge(s.aown, NE)
+    for h in halves:
+        g.vector.wait_ge(s["mmq%d" % h], 1)
+        g.vector.tensor_tensor(T.hp[:, col[h]], pq[h][:, 0:HALF], T.hown[:, col[h]], add).then_inc(s["cpq%d" % h], 1)
+    for h in halves:
+        g.tensor.wait_ge(s["cpq%d" % h], 1)
+        g.tensor.matmul(py[h][:, 0:HALF], T.xtm[:], T.hp[:, col[h]], start=False, stop=False)
+    g.tensor.wait_ge(s.aoth, NE)
+    for h in halves:
+        g.tensor.matmul(py[h][:, 0:HALF], T.xtm[:], T.hoth[:, col[h]], start=False, stop=True).then_inc(s["mmy%d" % h], 1)
+    for h in halves:
+        g.vector.wait_ge(s["mmy%d" % h], 1)
+        g.vector.tensor_tensor(T.ys[:, col[h]], py[h][:, 0:HALF], T.x15[:, col[h]], add).then_inc(s["yr%d" % h], 1)
+    for h in halves:
+        g.sync.wait_ge(s["yr%d" % h], 1)
     g.sync.dma_start(T.y[:], T.ys[:]).then_inc(s.st, 16)
     g.sync.wait_ge(s.st, 16)
-    g.wait_ge(s.sent, 2 * RANK_FAR + RANK_NEAR)
+    g.wait_ge(s.sent, 5 * NE)

from concourse.bass import DstId, RemoteDMATransfer
from concourse.mybir import AluOpType

D = 128
HALF = 64
WORLD = 256
NE = 8

SCRATCH = {
    "xd": ("dram", [D, D], "float32"),
    "xd0": ("dram", [D, D], "float32"),
    "xs": ("sbuf", [D, D], "float32"),
    "xts": ("sbuf", [D, D], "float32"),
    "xtm": ("sbuf", [D, D], "float32"),
    "cm": ("sbuf", [D, D], "float32"),
    "cp": ("sbuf", [D, D], "float32"),
    "x15": ("sbuf", [D, D], "float32"),
    "hs": ("sbuf", [D, D], "float32"),
    "lx1": ("sbuf", [D, D], "float32"),
    "lh0": ("sbuf", [D, D], "float32"),
    "land": ("sbuf", [D, D], "float32"),
    "xp": ("sbuf", [D, D], "float32"),
    "hp": ("sbuf", [D, D], "float32"),
    "hdir": ("sbuf", [D, D], "float32"),
    "hown": ("sbuf", [D, D], "float32"),
    "hoth": ("sbuf", [D, D], "float32"),
    "ys": ("sbuf", [D, D], "float32"),
    "pg": ("psum", [D, 512], "float32"),
    "pq0": ("psum", [D, 512], "float32"),
    "pq1": ("psum", [D, 512], "float32"),
    "py0": ("psum", [D, 512], "float32"),
    "py1": ("psum", [D, 512], "float32"),
}
SEMAPHORES = ["ldd", "ldx", "ldxt", "fill", "mm", "cpy", "sc", "sent", "arn", "arx", "arr", "arh", "axp", "adir",
              "mmq0", "mmq1", "cpq0", "cpq1", "aown", "aoth", "mmy0", "mmy1", "yr0", "yr1", "st"]


def _bits(mask, n, avoid=0):
    out, k = 0, 0
    for b in range(mask.bit_length()):
        if k < n and (mask >> b) & 1 and not (avoid >> b) & 1:
            out |= 1 << b
            k += 1
    return out


def _plan(T, topo):
    planes = []
    for c in T.cores:
        for p in planes:
            if topo.same_plane(p[0], c):
                p.append(c)
                break
        else:
            planes.append([c])
    a_side, b_side = planes
    partner = {}
    for a in a_side:
        for b in b_side:
            if topo.mates(a, b):
                partner[a], partner[b] = b, a
    rest_a = [a for a in a_side if a not in partner]
    rest_b = [b for b in b_side if b not in partner]
    for a, b in zip(rest_a, rest_b):
        partner[a], partner[b] = b, a
    red = {}
    for c in T.cores:
        red[c] = [w for w in range(WORLD)
                  if w != c and topo.host(w) == topo.host(c) and topo.chip(w) == topo.chip(c)
                  and topo.die(w) == topo.die(c) and topo.may_write(w, partner[c])][0]
    return planes, partner, red


def _send(g, topo, core, dst, out, src, rsem, lsem, mask):
    rid, pid = topo.addr(dst, core)
    g.remote_dma(out, src, rsem, lsem, pid, rid, mask)


def _fold(g, topo, core, dst, out, srcs, rsem, lsem, mask):
    rid, pid = topo.addr(dst, core)
    g.remote_dma_fused([RemoteDMATransfer(dst_ids=[DstId(rid=rid, pnc=pid)], dma_engine_mask=mask, remote_sem=rsem,
                                          srcs=srcs, dsts=[out], alu_op=1)], local_sem=lsem)


def rank_program(g, core, T, topo):
    planes, partner, red = _plan(T, topo)
    s = T.sem
    owner = {red[c]: c for c in T.cores}
    mult, add = AluOpType.mult, AluOpType.add

    if core in owner:
        mine = owner[core]
        plane = [p for p in planes if mine in p][0]
        n = len(plane)
        ahead = plane[(plane.index(mine) + n - 1) % n]
        far = topo.mask(core, partner[mine])
        m_far = _bits(far, NE)
        m_near = _bits(topo.mask(core, mine), NE, avoid=far)
        g.wait_ge(s.arn, NE)
        _send(g, topo, core, partner[ahead], T.xp[:], T.xd0[:], s.axp, s.sent, m_far)
        g.tensor.wait_ge(s.arx, NE)
        g.tensor.matmul(T.pg[:, 0:D], T.lx1[:], T.lx1[:], start=True, stop=True).then_inc(s.mm, 1)
        g.vector.wait_ge(s.arh, NE)
        g.vector.wait_ge(s.mm, 1)
        g.vector.tensor_tensor(T.hs[:], T.pg[:, 0:D], T.lh0[:], add).then_inc(s.cpy, 1)
        srcs = [T.hs[:], T.land[:]]
        g.wait_ge(s.cpy, 1)
        g.wait_ge(s.arr, NE)
        _fold(g, topo, core, partner[mine], T.hoth[:], srcs, s.aoth, s.sent, m_far)
        _fold(g, topo, core, mine, T.hown[:], srcs, s.aown, s.sent, m_near)
        g.wait_ge(s.sent, 3 * NE)
        return

    if T.rank_of(core) is None:
        return

    plane = [p for p in planes if core in p][0]
    me = plane.index(core)
    n = len(plane)
    away = [plane[(me + k) % n] for k in range(1, n)]
    far = topo.mask(core, red[away[0]])
    m_far = _bits(far, NE)
    m_near = _bits(topo.mask(core, red[core]), NE, avoid=far)

    g.sync.dma_start(T.xd[:], T.x[:]).then_inc(s.ldd, 16)
    g.scalar.dma_start(T.xs[:], T.x[:]).then_inc(s.ldx, 16)
    g.sync.dma_start(T.xts[:], T.xt[:]).then_inc(s.ldxt, 16)
    g.vector.memset(T.cm[:], -0.5).then_inc(s.fill, 1)
    g.vector.memset(T.cp[:], 1.5).then_inc(s.fill, 1)

    g.wait_ge(s.ldd, 16)
    _send(g, topo, core, red[core], T.xd0[:], T.xd[:], s.arn, s.sent, m_far)
    _send(g, topo, core, red[away[0]], T.lx1[:], T.xd[:], s.arx, s.sent, m_far)

    g.tensor.wait_ge(s.ldx, 16)
    g.tensor.matmul(T.pg[:, 0:D], T.xs[:], T.xs[:], start=True, stop=True).then_inc(s.mm, 1)
    g.vector.wait_ge(s.mm, 1)
    g.vector.tensor_copy(T.hs[:], T.pg[:, 0:D]).then_inc(s.cpy, 1)

    g.wait_ge(s.cpy, 1)
    _send(g, topo, core, red[away[1]], T.land[:], T.hs[:], s.arr, s.sent, m_far)
    _send(g, topo, core, red[core], T.lh0[:], T.hs[:], s.arh, s.sent, m_near)
    _send(g, topo, core, away[2], T.hdir[:], T.hs[:], s.adir, s.sent, m_far)

    g.vector.wait_ge(s.fill, 2)
    g.vector.wait_ge(s.ldxt, 16)
    g.vector.tensor_tensor(T.xtm[:], T.xts[:], T.cm[:], mult).then_inc(s.sc, 1)
    g.vector.wait_ge(s.ldx, 16)
    g.vector.tensor_tensor(T.x15[:], T.xs[:], T.cp[:], mult).then_inc(s.sc, 1)

    halves = (0, 1)
    col = [slice(h * HALF, (h + 1) * HALF) for h in halves]
    pq = [T.pq0, T.pq1]
    py = [T.py0, T.py1]
    g.tensor.wait_ge(s.sc, 2)
    g.tensor.wait_ge(s.adir, NE)
    for h in halves:
        g.tensor.matmul(py[h][:, 0:HALF], T.xtm[:], T.hdir[:, col[h]], start=True, stop=False)
    g.tensor.wait_ge(s.axp, NE)
    for h in halves:
        g.tensor.matmul(pq[h][:, 0:HALF], T.xp[:], T.xp[:, col[h]], start=True, stop=True).then_inc(s["mmq%d" % h], 1)
    g.vector.wait_ge(s.aown, NE)
    for h in halves:
        g.vector.wait_ge(s["mmq%d" % h], 1)
        g.vector.tensor_tensor(T.hp[:, col[h]], pq[h][:, 0:HALF], T.hown[:, col[h]], add).then_inc(s["cpq%d" % h], 1)
    for h in halves:
        g.tensor.wait_ge(s["cpq%d" % h], 1)
        g.tensor.matmul(py[h][:, 0:HALF], T.xtm[:], T.hp[:, col[h]], start=False, stop=False)
    g.tensor.wait_ge(s.aoth, NE)
    for h in halves:
        g.tensor.matmul(py[h][:, 0:HALF], T.xtm[:], T.hoth[:, col[h]], start=False, stop=True).then_inc(s["mmy%d" % h], 1)
    for h in halves:
        g.vector.wait_ge(s["mmy%d" % h], 1)
        g.vector.tensor_tensor(T.ys[:, col[h]], py[h][:, 0:HALF], T.x15[:, col[h]], add).then_inc(s["yr%d" % h], 1)
    for h in halves:
        g.sync.wait_ge(s["yr%d" % h], 1)
    g.sync.dma_start(T.y[:], T.ys[:]).then_inc(s.st, 16)
    g.sync.wait_ge(s.st, 16)
    g.wait_ge(s.sent, 5 * NE)
